import numpy as np
CORES = [1,2,9,10,17,18,25,26,33,34,41,42,49,50,57,58,65,66,73,74,81,82,89,90,97,98,105,106,113,114,121,122]
N = 32
PERM = [[0,28],[1,12],[2,16],[3,27],[4,1],[5,13],[6,18],[7,20],[8,9],[9,15],[10,30],[11,14],[12,6],[13,23],[14,24],[15,26],[16,3],[17,21],[18,25],[19,19],[20,5],[21,11],[22,17],[23,22],[24,10],[25,4],[26,8],[27,2],[28,31],[29,0],[30,7],[31,29]]
def setup_inputs(rng):
    return {"x": rng.standard_normal((N, 128, 1024), dtype=np.float32)}
def reference(x):
    y = np.empty_like(x)
    for s, d in PERM:
        y[d] = x[s]
    return {"y": y}

@@ -1,0 +1,47 @@
+SCRATCH = {
+    "stage": ("sbuf", [128, 1024], "float32"),
+    "land": ("sbuf", [128, 1024], "float32"),
+}
+SEMAPHORES = ["loaded", "sent", "arrived", "stored"]
+
+
+def route(topo, a, b):
+    if topo.may_write(a, b):
+        return [a, b]
+    return [a, (a // 8) * 8 + 6, b]
+
+
+def rank_program(g, core, T, topo):
+    cores = T.cores
+    routes = [route(topo, cores[s], cores[d]) for s, d in T.tables["PERM"] if s != d]
+    selfs = [cores[s] for s, d in T.tables["PERM"] if s == d]
+
+    def send(src_buf, dst):
+        rid, pid, _se = topo.addr(dst)
+        m = topo.mask(core, dst)
+        g.remote_dma(T.land[:], src_buf[:], T.sem.arrived, T.sem.sent, pid, rid, m)
+        return 16 if m == 0xFFFF else 8
+
+    if core in selfs:
+        g.dma_start(T.y[:], T.x[:]).then_inc(T.sem.stored, 16)
+        g.wait_ge(T.sem.stored, 16)
+        return
+
+    out_n = 0
+    for r in routes:
+        if r[0] == core:
+            g.dma_start(T.stage[:], T.x[:]).then_inc(T.sem.loaded, 16)
+            g.wait_ge(T.sem.loaded, 16)
+            out_n = send(T.stage, r[1])
+    for r in routes:
+        for i in range(1, len(r)):
+            if r[i] == core:
+                n = 16 if topo.mask(r[i - 1], core) == 0xFFFF else 8
+                g.wait_ge(T.sem.arrived, n)
+                if i == len(r) - 1:
+                    g.dma_start(T.y[:], T.land[:]).then_inc(T.sem.stored, 16)
+                    g.wait_ge(T.sem.stored, 16)
+                else:
+                    out_n = send(T.land, r[i + 1])
+    if out_n:
+        g.wait_ge(T.sem.sent, out_n)

@@ -1,47 +1,81 @@
+HALVES = 2
+ROWS = 128 // HALVES
+
 SCRATCH = {
-    "stage": ("sbuf", [128, 1024], "float32"),
-    "land": ("sbuf", [128, 1024], "float32"),
+    "out": ("dram", [HALVES, 128, 1024 // HALVES], "float32"),
+    "land": ("dram", [HALVES, 128, 1024 // HALVES], "float32"),
 }
-SEMAPHORES = ["loaded", "sent", "arrived", "stored"]
+SEMAPHORES = ["ld0", "ld1", "arr0", "arr1", "st0", "st1", "sent"]
 
 
-def route(topo, a, b):
-    if topo.may_write(a, b):
-        return [a, b]
-    return [a, (a // 8) * 8 + 6, b]
+def engines(mask):
+    return bin(mask).count("1")
+
+
+def relay_on(topo, group, a, b, die):
+    base = topo.chip(a) * 8
+    free = [c for c in range(base, base + 8) if c not in group and topo.die(c) == die and topo.may_write(c, b)]
+    mine = [c for c in group if topo.chip(c) == topo.chip(a)].index(a)
+    return free[len(free) - 1 - mine]
+
+
+def plan(T, topo):
+    group = list(T.cores)
+    ways, keep = [], []
+    for s, d in T.tables["PERM"]:
+        a, b = group[s], group[d]
+        if a == b:
+            keep.append(a)
+        elif topo.chip(a) == topo.chip(b):
+            ways += [(h, [a, b]) for h in range(HALVES)]
+        else:
+            own = topo.die(a)
+            ways.append((0, [a, b] if topo.may_write(a, b) else [a, relay_on(topo, group, a, b, own), b]))
+            ways.append((1, [a, relay_on(topo, group, a, b, 1 - own), b]))
+    landings = [(h, c) for h, way in ways for c in way[1:]]
+    if len(set(landings)) != len(landings):
+        raise ValueError("two halves would land in one slot")
+    return ways, keep
 
 
 def rank_program(g, core, T, topo):
-    cores = T.cores
-    routes = [route(topo, cores[s], cores[d]) for s, d in T.tables["PERM"] if s != d]
-    selfs = [cores[s] for s, d in T.tables["PERM"] if s == d]
+    ways, keep = plan(T, topo)
+    queue = [g.scalar, g.sync]
+    ld = [T.sem.ld0, T.sem.ld1]
+    arr = [T.sem.arr0, T.sem.arr1]
+    st = [T.sem.st0, T.sem.st1]
 
-    def send(src_buf, dst):
-        rid, pid, _se = topo.addr(dst)
-        m = topo.mask(core, dst)
-        g.remote_dma(T.land[:], src_buf[:], T.sem.arrived, T.sem.sent, pid, rid, m)
-        return 16 if m == 0xFFFF else 8
-
-    if core in selfs:
-        g.dma_start(T.y[:], T.x[:]).then_inc(T.sem.stored, 16)
-        g.wait_ge(T.sem.stored, 16)
+    if core in keep:
+        g.sync.dma_start(T.y[:], T.x[:]).then_inc(st[0], 16)
+        g.sync.wait_ge(st[0], 16)
         return
 
-    out_n = 0
-    for r in routes:
-        if r[0] == core:
-            g.dma_start(T.stage[:], T.x[:]).then_inc(T.sem.loaded, 16)
-            g.wait_ge(T.sem.loaded, 16)
-            out_n = send(T.stage, r[1])
-    for r in routes:
-        for i in range(1, len(r)):
-            if r[i] == core:
-                n = 16 if topo.mask(r[i - 1], core) == 0xFFFF else 8
-                g.wait_ge(T.sem.arrived, n)
-                if i == len(r) - 1:
-                    g.dma_start(T.y[:], T.land[:]).then_inc(T.sem.stored, 16)
-                    g.wait_ge(T.sem.stored, 16)
-                else:
-                    out_n = send(T.land, r[i + 1])
-    if out_n:
-        g.wait_ge(T.sem.sent, out_n)
+    def write(h, src, dst):
+        rid, pid, _ring = topo.addr(dst)
+        mask = topo.mask(core, dst)
+        g.remote_dma(T.land[h], src[h], arr[h], T.sem.sent, pid, rid, mask)
+        return engines(mask)
+
+    leaving = sorted([w for w in ways if w[1][0] == core], key=lambda w: (-len(w[1]), w[0]))
+    passing = [w for w in ways if core in w[1][1:-1]]
+    coming = [w for w in ways if w[1][-1] == core]
+    sent = 0
+
+    for h, way in leaving:
+        queue[h].dma_start(T.out[h], T.x[h * ROWS:(h + 1) * ROWS, :]).then_inc(ld[h], 16)
+    for h, way in leaving:
+        g.wait_ge(ld[h], 16)
+        sent += write(h, T.out, way[1])
+
+    for h, way in passing:
+        i = way.index(core)
+        g.wait_ge(arr[h], engines(topo.mask(way[i - 1], core)))
+        sent += write(h, T.land, way[i + 1])
+
+    for h, way in coming:
+        queue[h].wait_ge(arr[h], engines(topo.mask(way[-2], core)))
+        queue[h].dma_start(T.y[h * ROWS:(h + 1) * ROWS, :], T.land[h]).then_inc(st[h], 16)
+        queue[h].wait_ge(st[h], 16)
+
+    if sent:
+        g.wait_ge(T.sem.sent, sent)

HALVES = 2
ROWS = 128 // HALVES

SCRATCH = {
    "out": ("dram", [HALVES, 128, 1024 // HALVES], "float32"),
    "land": ("dram", [HALVES, 128, 1024 // HALVES], "float32"),
}
SEMAPHORES = ["ld0", "ld1", "arr0", "arr1", "st0", "st1", "sent"]


def engines(mask):
    return bin(mask).count("1")


def relay_on(topo, group, a, b, die):
    base = topo.chip(a) * 8
    free = [c for c in range(base, base + 8) if c not in group and topo.die(c) == die and topo.may_write(c, b)]
    mine = [c for c in group if topo.chip(c) == topo.chip(a)].index(a)
    return free[len(free) - 1 - mine]


def plan(T, topo):
    group = list(T.cores)
    ways, keep = [], []
    for s, d in T.tables["PERM"]:
        a, b = group[s], group[d]
        if a == b:
            keep.append(a)
        elif topo.chip(a) == topo.chip(b):
            ways += [(h, [a, b]) for h in range(HALVES)]
        else:
            own = topo.die(a)
            ways.append((0, [a, b] if topo.may_write(a, b) else [a, relay_on(topo, group, a, b, own), b]))
            ways.append((1, [a, relay_on(topo, group, a, b, 1 - own), b]))
    landings = [(h, c) for h, way in ways for c in way[1:]]
    if len(set(landings)) != len(landings):
        raise ValueError("two halves would land in one slot")
    return ways, keep


def rank_program(g, core, T, topo):
    ways, keep = plan(T, topo)
    queue = [g.scalar, g.sync]
    ld = [T.sem.ld0, T.sem.ld1]
    arr = [T.sem.arr0, T.sem.arr1]
    st = [T.sem.st0, T.sem.st1]

    if core in keep:
        g.sync.dma_start(T.y[:], T.x[:]).then_inc(st[0], 16)
        g.sync.wait_ge(st[0], 16)
        return

    def write(h, src, dst):
        rid, pid, _ring = topo.addr(dst)
        mask = topo.mask(core, dst)
        g.remote_dma(T.land[h], src[h], arr[h], T.sem.sent, pid, rid, mask)
        return engines(mask)

    leaving = sorted([w for w in ways if w[1][0] == core], key=lambda w: (-len(w[1]), w[0]))
    passing = [w for w in ways if core in w[1][1:-1]]
    coming = [w for w in ways if w[1][-1] == core]
    sent = 0

    for h, way in leaving:
        queue[h].dma_start(T.out[h], T.x[h * ROWS:(h + 1) * ROWS, :]).then_inc(ld[h], 16)
    for h, way in leaving:
        g.wait_ge(ld[h], 16)
        sent += write(h, T.out, way[1])

    for h, way in passing:
        i = way.index(core)
        g.wait_ge(arr[h], engines(topo.mask(way[i - 1], core)))
        sent += write(h, T.land, way[i + 1])

    for h, way in coming:
        queue[h].wait_ge(arr[h], engines(topo.mask(way[-2], core)))
        queue[h].dma_start(T.y[h * ROWS:(h + 1) * ROWS, :], T.land[h]).then_inc(st[h], 16)
        queue[h].wait_ge(st[h], 16)

    if sent:
        g.wait_ge(T.sem.sent, sent)
